import numpy as np, ml_dtypes
CORES = [100,101,102,103,108,109,110,111]
N = 8
import mx_ref
NC, G = 128, 4
C = np.float32(0.023)
BF = ml_dtypes.bfloat16
def cut(t, i, w=512):
    return t[:, w * i:w * i + w]
def tile(rs):
    return np.stack(rs, axis=2).reshape(128, -1).astype(BF)
def layer(w, X):
    out = []
    for i in range(G):
        for t in range(len(X)):
            p = mx_ref.matmul(mx_ref.quantize(cut(w, len(X) * i + t)), X[t])
            z = p if t == 0 else z + p
        out.append(z)
    return out
def act(Z):
    return [np.maximum(z, 0) * C for z in Z]
def setup_inputs(rng):
    def f(*shape):
        return mx_ref.flush((rng.standard_normal(shape, dtype=np.float32) * np.exp2(rng.integers(-2, 3, shape[:-1] + (1,)))).astype(BF))
    return {"x": f(N, 128, 4 * NC), "w1": f(N, 128, G * 512), "w2": f(N, 128, 512)}
def setup_inputs_blocks(rng):
    d = setup_inputs(rng)
    for k in ("x", "w1", "w2"): d[k] = mx_ref.spread(d[k], rng, 2)
    return d
def setup_inputs_wide(rng):
    d = setup_inputs(rng)
    for k in ("x", "w1", "w2"): d[k] = mx_ref.flush((d[k].astype(np.float32) * np.exp2(rng.integers(-6, 7, (N, 1, 1))).astype(np.float32)).astype(BF))
    return d
def reference(x, w1, w2):
    X = [mx_ref.quantize(x[j]) for j in range(N)]
    y = np.zeros((N, 128, NC), np.float32)
    for c in range(N):
        for r in range(N):
            p = mx_ref.matmul(mx_ref.quantize(w2[r]), mx_ref.quantize(tile(act(layer(w1[r], [X[c]])))))
            y[c] = p if r == 0 else y[c] + p
    return {"y": y}

@@ -1,0 +1,299 @@
+import numpy as np
+from concourse.bass import DstId, RemoteDMATransfer
+from concourse.mybir import dt, AluOpType, ActivationFunctionType
+
+NT = 128
+G = 4
+REG = (G + 1) * NT
+CH = [3, 2]
+NCH = len(CH)
+C = float(np.float32(0.023))
+
+SCRATCH = {
+    "xb": ("sbuf", [128, 4 * NT], "bfloat16"),
+    "w2b": ("sbuf", [128, 4 * NT], "bfloat16"),
+    "w1b": ("sbuf", [128, 4 * NT * G], "bfloat16"),
+    "xq": ("sbuf", [128, 4 * NT], "float8_e4m3fn_x4"), "xs": ("sbuf", [128, 4 * NT], "uint8"),
+    "wq": ("sbuf", [128, 2 * REG], "float8_e4m3fn_x4"), "ws": ("sbuf", [128, 2 * REG], "uint8"),
+    "rq": ("sbuf", [128, 4 * REG], "float8_e4m3fn_x4"), "rs": ("sbuf", [128, 4 * REG], "uint8"),
+    "pq": ("sbuf", [128, 8 * NT], "float8_e4m3fn_x4"), "ps": ("sbuf", [128, 8 * NT], "uint8"),
+    "hb0": ("sbuf", [128, 16 * NT], "bfloat16"), "hb1": ("sbuf", [128, 16 * NT], "bfloat16"),
+    "hq0": ("sbuf", [128, 4 * NT], "float8_e4m3fn_x4"), "hs0": ("sbuf", [128, 4 * NT], "uint8"),
+    "hq1": ("sbuf", [128, 4 * NT], "float8_e4m3fn_x4"), "hs1": ("sbuf", [128, 4 * NT], "uint8"),
+    "hin": ("sbuf", [128, 8 * NT], "float8_e4m3fn_x4"), "his": ("sbuf", [128, 8 * NT], "uint8"),
+    "ysb": ("sbuf", [128, NT], "float32"),
+    "z": ("psum", [128, 8 * 512], "float32"),
+}
+SEMAPHORES = (["ld_x", "ld_w2", "q_x", "q_w2", "a_x", "a_p", "a_ho", "af0", "af1", "y_mm", "y_cp", "y_st", "sent"]
+              + ["ld_w1_%d" % j for j in range(NCH)] + ["q_w1_%d" % j for j in range(NCH)]
+              + ["a_hc%d" % p for p in range(4)]
+              + ["c%d_%d" % (i, j) for i in range(4) for j in range(NCH)]
+              + ["z0_%d" % a for a in range(4)] + ["z1_%d" % a for a in range(3)] + ["zd%d" % a for a in range(4)]
+              + ["al%d_%d" % (t, c) for t in range(2) for c in range(4)]
+              + ["qh%d_%d" % (t, c) for t in range(2) for c in range(4)])
+
+
+def _nb(m):
+    return bin(m).count("1")
+
+
+def _units(j):
+    m0 = sum(CH[:j])
+    return m0, m0 + CH[j]
+
+
+def _ucol(s, m):
+    return REG - NT * (m + 1) if s == 0 else REG + NT * m
+
+
+def _utile(s, m):
+    return G - m if s == 0 else m - 1
+
+
+def _ccols(s, j):
+    m0, m1 = _units(j)
+    return (REG - NT * m1, REG - NT * m0) if s == 0 else (REG + NT * m0, REG + NT * m1)
+
+
+def _ctiles(s, j):
+    m0, m1 = _units(j)
+    t = [_utile(s, m) for m in range(max(m0, 1), m1)]
+    return (min(t), max(t) + 1) if t else None
+
+
+def _chunk_of(m):
+    for j in range(NCH):
+        m0, m1 = _units(j)
+        if m0 <= m < m1:
+            return j
+
+
+def _plan(T, topo):
+    cores = list(T.cores)
+    chips = []
+    for c in cores:
+        if topo.chip(c) not in chips:
+            chips.append(topo.chip(c))
+    grp = [[c for c in cores if topo.chip(c) == ch] for ch in chips]
+    side, idx, partner, route, fwd = {}, {}, {}, {}, {}
+    for s in (0, 1):
+        for i, c in enumerate(grp[s]):
+            side[c], idx[c], partner[c] = s, i, grp[1 - s][i]
+    for s in (0, 1):
+        free = [h for h in range(topo.CORES_PER_CHIP * topo.CHIPS)
+                if topo.chip(h) == chips[s] and h not in cores and topo.may_write(h, grp[1 - s][0])]
+        for c in grp[s]:
+            if topo.may_write(c, partner[c]):
+                path = [c, partner[c]]
+            else:
+                free.sort(key=lambda h: topo.die(h) == topo.die(c))
+                path = [c, free.pop(0), partner[c]]
+            for j in range(NCH):
+                route[(c, j)] = path
+    for j in range(NCH):
+        for c in cores:
+            p = route[(c, j)]
+            for k in range(1, len(p) - 1):
+                fwd.setdefault(p[k], []).append((c, j, p[k - 1], p[k + 1]))
+    return {"grp": grp, "side": side, "idx": idx, "partner": partner, "route": route, "fwd": fwd}
+
+
+def rank_program(g, core, T, topo):
+    P = _plan(T, topo)
+    side, idx, partner, route = P["side"], P["idx"], P["partner"], P["route"]
+    jobs = P["fwd"].get(core, [])
+    rank = T.rank_of(core)
+    if rank is None and not jobs:
+        return
+    S = T.sem
+    u8 = dt.uint8
+    sent = [0]
+
+    def send(dst, out_ap, in_ap, rsem):
+        rid, pid, _ = topo.addr(dst)
+        m = topo.mask(core, dst)
+        g.remote_dma(out_ap=out_ap, in_ap=in_ap, remote_sem=rsem, local_sem=S.sent, pid=pid, routing_id=rid,
+                     dma_engine_mask=m)
+        sent[0] += _nb(m)
+
+    def did(d):
+        rid, pid, _ = topo.addr(d)
+        return DstId(rid=rid, pnc=pid)
+
+    def multi(dsts, out_ap, in_ap, rsem):
+        m = topo.mask(core, dsts[0])
+        g.remote_dma_fused([RemoteDMATransfer(dst_ids=[did(d) for d in dsts], dma_engine_mask=m, remote_sem=rsem,
+                                              srcs=[in_ap], dsts=[out_ap] * len(dsts))], local_sem=S.sent)
+        sent[0] += _nb(m)
+
+    def hop(src, j, nxt, from_stage):
+        s = side[src]
+        a, b = _ccols(s, j)
+        off = REG * idx[src] - REG * s
+        sem = S["c%d_%d" % (idx[src], j)]
+        iq, isc = (T.rq[:, a + off:b + off], T.rs[:, a + off:b + off]) if from_stage else (T.wq[:, a:b], T.ws[:, a:b])
+        if nxt == partner[src]:
+            oq, osc = T.wq[:, a:b], T.ws[:, a:b]
+        else:
+            oq, osc = T.rq[:, a + off:b + off], T.rs[:, a + off:b + off]
+        send(nxt, oq.bitcast(u8), iq.bitcast(u8), sem)
+        send(nxt, osc, isc, sem)
+
+    def forward():
+        for (src, j, prev, nxt) in jobs:
+            g.wait_ge(S["c%d_%d" % (idx[src], j)], 2 * _nb(topo.mask(prev, core)))
+            hop(src, j, nxt, True)
+
+    if rank is None:
+        forward()
+        g.wait_ge(S.sent, sent[0])
+        return
+
+    s, k = side[core], idx[core]
+    o = 1 - s
+    peers = [c for c in P["grp"][s] if c != core]
+    order = [(k + 1 + i) % 4 for i in range(4)]
+    te, ve, sc, sy = g.tensor, g.vector, g.scalar, g.sync
+    ksl = slice(NT * k, NT * k + NT)
+    ccnt = [2 * _nb(topo.mask(route[(partner[core], j)][-2], core)) for j in range(NCH)]
+    csem = [S["c%d_%d" % (k, j)] for j in range(NCH)]
+
+    sy.dma_start(T.xb[:], T.x[:]).then_inc(S.ld_x, 16)
+    sc.dma_start(T.w2b[:], T.w2[:]).then_inc(S.ld_w2, 16)
+    for j in range(NCH):
+        t = _ctiles(s, j)
+        if t:
+            q = sy if j % 2 == 0 else sc
+            q.dma_start(T.w1b[:, 512 * t[0]:512 * t[1]], T.w1[:, 512 * t[0]:512 * t[1]]).then_inc(S["ld_w1_%d" % j], 16)
+
+    ve.wait_ge(S.ld_x, 16)
+    ve.quantize_mx(T.xq[:, ksl], T.xs[:, ksl], T.xb[:]).then_inc(S.q_x, 1)
+    ve.wait_ge(S.ld_w2, 16)
+    w2c = _ucol(s, 0)
+    ve.quantize_mx(T.wq[:, w2c:w2c + NT], T.ws[:, w2c:w2c + NT], T.w2b[:]).then_inc(S.q_w2, 1)
+    for j in range(NCH):
+        t = _ctiles(s, j)
+        if t:
+            a = _ucol(s, 1) + NT * (t[0] - _utile(s, 1))
+            b = a + NT * (t[1] - t[0])
+            ve.wait_ge(S["ld_w1_%d" % j], 16)
+            ve.quantize_mx(T.wq[:, a:b], T.ws[:, a:b], T.w1b[:, 512 * t[0]:512 * t[1]]).then_inc(S["q_w1_%d" % j], 1)
+
+    te.wait_ge(S.q_x, 1)
+    te.wait_ge(S.a_x, sum(2 * _nb(topo.mask(p, core)) for p in peers))
+    for a in range(4):
+        te.wait_ge(S["q_w1_%d" % _chunk_of(a + 1)], 1)
+        col = _ucol(s, a + 1)
+        te.matmul_mx(T.z[:, 512 * a:512 * a + 512], T.wq[:, col:col + NT], T.ws[:, col:col + NT], T.xq[:], T.xs[:],
+                     True, True).then_inc(S["z0_%d" % a], 1)
+    for a in range(3):
+        j = _chunk_of(a + 1)
+        te.wait_ge(csem[j], ccnt[j])
+        col = _ucol(o, a + 1)
+        te.matmul_mx(T.z[:, 512 * (4 + a):512 * (4 + a) + 512], T.wq[:, col:col + NT], T.ws[:, col:col + NT],
+                     T.xq[:], T.xs[:], True, True).then_inc(S["z1_%d" % a], 1)
+    te.wait_ge(S.af0, 3)
+    for c in range(4):
+        te.wait_ge(S["al0_%d" % c], 1)
+    te.wait_ge(csem[NCH - 1], ccnt[NCH - 1])
+    col = _ucol(o, 4)
+    for i, c in enumerate(order):
+        te.matmul_mx(T.z[:, 512 * i:512 * i + NT], T.wq[:, col:col + NT], T.ws[:, col:col + NT],
+                     T.xq[:, NT * c:NT * c + NT], T.xs[:, NT * c:NT * c + NT], True, True).then_inc(S["zd%d" % i], 1)
+
+    for st in range(2):
+        hb, hq, hs = T["hb%d" % st], T["hq%d" % st], T["hs%d" % st]
+        reg = s if st == 0 else o
+        bank = 0 if st == 0 else 4
+        af = S["af%d" % st]
+        for a, eng in ((0, ve), (1, sc), (2, ve)):
+            b = _utile(reg, a + 1)
+            eng.wait_ge(S["z%d_%d" % (st, a)], 1)
+            zin = T.z[:, 512 * (bank + a):512 * (bank + a) + 512]
+            if eng is ve:
+                ve.tensor_scalar(hb[:, b:16 * NT:4], zin, 0.0, C, AluOpType.max, AluOpType.mult).then_inc(af, 1)
+            else:
+                sc.activation(hb[:, b:16 * NT:4], zin, ActivationFunctionType.Relu, scale=C).then_inc(af, 1)
+        b = _utile(reg, 4)
+        if st == 0:
+            sc.wait_ge(S.z0_3, 1)
+        for i, c in enumerate(order):
+            if st == 0:
+                zin = T.z[:, 512 * 3 + NT * c:512 * 3 + NT * c + NT]
+            else:
+                sc.wait_ge(S["zd%d" % i], 1)
+                zin = T.z[:, 512 * i:512 * i + NT]
+            sc.activation(hb[:, 512 * c + b:512 * c + 512:4], zin, ActivationFunctionType.Relu,
+                          scale=C).then_inc(S["al%d_%d" % (st, c)], 1)
+        ve.wait_ge(af, 3)
+        for c in order:
+            ve.wait_ge(S["al%d_%d" % (st, c)], 1)
+            ve.quantize_mx(hq[:, NT * c:NT * c + NT], hs[:, NT * c:NT * c + NT],
+                           hb[:, 512 * c:512 * c + 512]).then_inc(S["qh%d_%d" % (st, c)], 1)
+
+    full = topo.mask(core, peers[0])
+    eng = [e for e in range(full.bit_length()) if (full >> e) & 1]
+    n = len(eng)
+
+    def mk(lo, hi):
+        return sum(1 << e for e in eng[lo:hi])
+    mq = [mk(0, n // 2), mk(n // 2, 3 * n // 4), mk(3 * n // 4, n)]
+    ms = [mk(0, n // 4), mk(n // 4, n // 2), mk(n // 2, n)]
+    hcnt = [_nb(mq[i]) + _nb(ms[i]) for i in range(3)]
+
+    yb = T.z[:, 512 * 7:512 * 7 + NT]
+    L2 = []
+    xc = _ucol(o, 0)
+    L2.append(([(S.q_w2, 1), (S["qh0_%d" % k], 1)], T.wq[:, w2c:w2c + NT], T.ws[:, w2c:w2c + NT], T.hq0[:, ksl], T.hs0[:, ksl]))
+    for n_, pc in enumerate(peers):
+        p = idx[pc]
+        w = [(S.a_p, sum(2 * _nb(topo.mask(q, core)) for q in peers)), (S.a_ho, sum(hcnt))] if n_ == 0 else []
+        a, h = 2 * NT * p + NT * s, 2 * NT * p
+        L2.append((w, T.pq[:, a:a + NT], T.ps[:, a:a + NT], T.hin[:, h:h + NT], T.his[:, h:h + NT]))
+    L2.append(([(csem[0], ccnt[0]), (S["qh1_%d" % k], 1)], T.wq[:, xc:xc + NT], T.ws[:, xc:xc + NT], T.hq1[:, ksl], T.hs1[:, ksl]))
+    for pc in peers:
+        p = idx[pc]
+        a, h = 2 * NT * p + NT * o, 2 * NT * p + NT
+        L2.append(([(S["a_hc%d" % p], hcnt[(k - p - 1) % 4])], T.pq[:, a:a + NT], T.ps[:, a:a + NT],
+                   T.hin[:, h:h + NT], T.his[:, h:h + NT]))
+    for i, (w, wq_, ws_, hq_, hs_) in enumerate(L2):
+        for sem, v in w:
+            te.wait_ge(sem, v)
+        ins = te.matmul_mx(yb, wq_, ws_, hq_, hs_, i == 0, i == len(L2) - 1)
+        if i == len(L2) - 1:
+            ins.then_inc(S.y_mm, 1)
+    ve.wait_ge(S.y_mm, 1)
+    ve.tensor_copy(T.ysb[:], yb).then_inc(S.y_cp, 1)
+    sy.wait_ge(S.y_cp, 1)
+    sy.dma_start(T.y[:], T.ysb[:]).then_inc(S.y_st, 16)
+    sy.wait_ge(S.y_st, 16)
+
+    g.wait_ge(S.q_x, 1)
+    multi(peers, T.xq[:, ksl].bitcast(u8), T.xq[:, ksl].bitcast(u8), S.a_x)
+    multi(peers, T.xs[:, ksl], T.xs[:, ksl], S.a_x)
+    for j in range(NCH):
+        if j == 0:
+            g.wait_ge(S.q_w2, 1)
+        if _ctiles(s, j):
+            g.wait_ge(S["q_w1_%d" % j], 1)
+        hop(core, j, route[(core, j)][1], False)
+    forward()
+    g.wait_ge(csem[0], ccnt[0])
+    pa = 2 * NT * k
+    multi(peers, T.pq[:, pa:pa + 2 * NT].bitcast(u8), T.wq[:, REG - NT:REG + NT].bitcast(u8), S.a_p)
+    multi(peers, T.ps[:, pa:pa + 2 * NT], T.ws[:, REG - NT:REG + NT], S.a_p)
+    for st in range(2):
+        hq, hs = T["hq%d" % st], T["hs%d" % st]
+        rsem = S.a_ho if st == 0 else S["a_hc%d" % k]
+        for c in order[:3]:
+            g.wait_ge(S["qh%d_%d" % (st, c)], 1)
+        h = 2 * NT * k + NT * st
+        g.remote_dma_fused([RemoteDMATransfer(dst_ids=[did(P["grp"][s][c])], dma_engine_mask=mq[i], remote_sem=rsem,
+                                              src=hq[:, NT * c:NT * c + NT].bitcast(u8),
+                                              dst=T.hin[:, h:h + NT].bitcast(u8))
+                            for i, c in enumerate(order[:3])], local_sem=S.sent)
+        g.remote_dma_fused([RemoteDMATransfer(dst_ids=[did(P["grp"][s][c])], dma_engine_mask=ms[i], remote_sem=rsem,
+                                              src=hs[:, NT * c:NT * c + NT], dst=T.his[:, h:h + NT])
+                            for i, c in enumerate(order[:3])], local_sem=S.sent)
+        sent[0] += sum(hcnt)
+    g.wait_ge(S.sent, sent[0])

@@ -5,7 +5,7 @@ from concourse.mybir import dt, AluOpType, ActivationFunctionType
 NT = 128
 G = 4
 REG = (G + 1) * NT
-CH = [3, 2]
+CH = [1, 2, 2]
 NCH = len(CH)
 C = float(np.float32(0.023))
 
@@ -166,11 +166,11 @@ def rank_program(g, core, T, topo):
             q = sy if j % 2 == 0 else sc
             q.dma_start(T.w1b[:, 512 * t[0]:512 * t[1]], T.w1[:, 512 * t[0]:512 * t[1]]).then_inc(S["ld_w1_%d" % j], 16)
 
-    ve.wait_ge(S.ld_x, 16)
-    ve.quantize_mx(T.xq[:, ksl], T.xs[:, ksl], T.xb[:]).then_inc(S.q_x, 1)
     ve.wait_ge(S.ld_w2, 16)
     w2c = _ucol(s, 0)
     ve.quantize_mx(T.wq[:, w2c:w2c + NT], T.ws[:, w2c:w2c + NT], T.w2b[:]).then_inc(S.q_w2, 1)
+    ve.wait_ge(S.ld_x, 16)
+    ve.quantize_mx(T.xq[:, ksl], T.xs[:, ksl], T.xb[:]).then_inc(S.q_x, 1)
     for j in range(NCH):
         t = _ctiles(s, j)
         if t:
@@ -268,15 +268,16 @@ def rank_program(g, core, T, topo):
     sy.dma_start(T.y[:], T.ysb[:]).then_inc(S.y_st, 16)
     sy.wait_ge(S.y_st, 16)
 
-    g.wait_ge(S.q_x, 1)
-    multi(peers, T.xq[:, ksl].bitcast(u8), T.xq[:, ksl].bitcast(u8), S.a_x)
-    multi(peers, T.xs[:, ksl], T.xs[:, ksl], S.a_x)
     for j in range(NCH):
         if j == 0:
             g.wait_ge(S.q_w2, 1)
         if _ctiles(s, j):
             g.wait_ge(S["q_w1_%d" % j], 1)
         hop(core, j, route[(core, j)][1], False)
+        if j == 0:
+            g.wait_ge(S.q_x, 1)
+            multi(peers, T.xq[:, ksl].bitcast(u8), T.xq[:, ksl].bitcast(u8), S.a_x)
+            multi(peers, T.xs[:, ksl], T.xs[:, ksl], S.a_x)
     forward()
     g.wait_ge(csem[0], ccnt[0])
     pa = 2 * NT * k

@@ -5,8 +5,9 @@ from concourse.mybir import dt, AluOpType, ActivationFunctionType
 NT = 128
 G = 4
 REG = (G + 1) * NT
-CH = [1, 2, 2]
-NCH = len(CH)
+CALLS = [[("q", 0, 1)], [("s", 0, 1)], [("q", 1, 2), ("s", 1, 5)], [("q", 2, 4)], [("q", 4, 5)]]
+NK = len(CALLS)
+LG = [(1, 3), (3, 5)]
 C = float(np.float32(0.023))
 
 SCRATCH = {
@@ -24,48 +25,41 @@ SCRATCH = {
     "ysb": ("sbuf", [128, NT], "float32"),
     "z": ("psum", [128, 8 * 512], "float32"),
 }
-SEMAPHORES = (["ld_x", "ld_w2", "q_x", "q_w2", "a_x", "a_p", "a_ho", "af0", "af1", "y_mm", "y_cp", "y_st", "sent"]
-              + ["ld_w1_%d" % j for j in range(NCH)] + ["q_w1_%d" % j for j in range(NCH)]
+SEMAPHORES = (["ld_x", "ld_w2", "q_x", "q_w2", "a_x", "a_p", "a_ho", "y_mm", "y_cp", "y_st", "sent",
+               "afC", "afA", "afB", "afD", "qhC", "qhA", "qhD"]
+              + ["ld_w1_%d" % j for j in range(len(LG))] + ["q_w1_%d" % j for j in range(len(LG))]
               + ["a_hc%d" % p for p in range(4)]
-              + ["c%d_%d" % (i, j) for i in range(4) for j in range(NCH)]
-              + ["z0_%d" % a for a in range(4)] + ["z1_%d" % a for a in range(3)] + ["zd%d" % a for a in range(4)]
-              + ["al%d_%d" % (t, c) for t in range(2) for c in range(4)]
-              + ["qh%d_%d" % (t, c) for t in range(2) for c in range(4)])
+              + ["c%d_%d" % (i, j) for i in range(4) for j in range(NK)]
+              + ["z%s%d" % (ph, a) for ph in "CAD" for a in range(4)] + ["zB%d" % a for a in range(3)]
+              + ["zL%d" % i for i in range(3)] + ["aL%d" % i for i in range(3)] + ["qhB%d" % i for i in range(3)])
 
 
 def _nb(m):
     return bin(m).count("1")
 
 
-def _units(j):
-    m0 = sum(CH[:j])
-    return m0, m0 + CH[j]
+def _engines(m):
+    return [e for e in range(m.bit_length()) if (m >> e) & 1]
 
 
-def _ucol(s, m):
-    return REG - NT * (m + 1) if s == 0 else REG + NT * m
+def _mk(es):
+    return sum(1 << e for e in es)
+
+
+def _cols(s, m0, m1):
+    return (REG - NT * m1, REG - NT * m0) if s == 0 else (REG + NT * m0, REG + NT * m1)
 
 
 def _utile(s, m):
     return G - m if s == 0 else m - 1
 
 
-def _ccols(s, j):
-    m0, m1 = _units(j)
-    return (REG - NT * m1, REG - NT * m0) if s == 0 else (REG + NT * m0, REG + NT * m1)
+def _need(m):
+    return [K for K, ps in enumerate(CALLS) if any(m0 <= m < m1 for (_, m0, m1) in ps)]
 
 
-def _ctiles(s, j):
-    m0, m1 = _units(j)
-    t = [_utile(s, m) for m in range(max(m0, 1), m1)]
-    return (min(t), max(t) + 1) if t else None
-
-
-def _chunk_of(m):
-    for j in range(NCH):
-        m0, m1 = _units(j)
-        if m0 <= m < m1:
-            return j
+def _group_of(m):
+    return [j for j, (m0, m1) in enumerate(LG) if m0 <= m < m1][0]
 
 
 def _plan(T, topo):
@@ -84,17 +78,15 @@ def _plan(T, topo):
                 if topo.chip(h) == chips[s] and h not in cores and topo.may_write(h, grp[1 - s][0])]
         for c in grp[s]:
             if topo.may_write(c, partner[c]):
-                path = [c, partner[c]]
+                route[c] = [c, partner[c]]
             else:
                 free.sort(key=lambda h: topo.die(h) == topo.die(c))
-                path = [c, free.pop(0), partner[c]]
-            for j in range(NCH):
-                route[(c, j)] = path
-    for j in range(NCH):
+                route[c] = [c, free.pop(0), partner[c]]
+    for K in range(NK):
         for c in cores:
-            p = route[(c, j)]
+            p = route[c]
             for k in range(1, len(p) - 1):
-                fwd.setdefault(p[k], []).append((c, j, p[k - 1], p[k + 1]))
+                fwd.setdefault(p[k], []).append((c, K, p[k - 1], p[k + 1]))
     return {"grp": grp, "side": side, "idx": idx, "partner": partner, "route": route, "fwd": fwd}
 
 
@@ -109,40 +101,51 @@ def rank_program(g, core, T, topo):
     u8 = dt.uint8
     sent = [0]
 
-    def send(dst, out_ap, in_ap, rsem):
-        rid, pid, _ = topo.addr(dst)
-        m = topo.mask(core, dst)
-        g.remote_dma(out_ap=out_ap, in_ap=in_ap, remote_sem=rsem, local_sem=S.sent, pid=pid, routing_id=rid,
-                     dma_engine_mask=m)
-        sent[0] += _nb(m)
-
     def did(d):
         rid, pid, _ = topo.addr(d)
         return DstId(rid=rid, pnc=pid)
 
-    def multi(dsts, out_ap, in_ap, rsem):
+    def multi(dsts, out_aps, in_ap, rsem):
         m = topo.mask(core, dsts[0])
         g.remote_dma_fused([RemoteDMATransfer(dst_ids=[did(d) for d in dsts], dma_engine_mask=m, remote_sem=rsem,
-                                              srcs=[in_ap], dsts=[out_ap] * len(dsts))], local_sem=S.sent)
+                                              srcs=[in_ap], dsts=out_aps)], local_sem=S.sent)
         sent[0] += _nb(m)
 
-    def hop(src, j, nxt, from_stage):
-        s = side[src]
-        a, b = _ccols(s, j)
-        off = REG * idx[src] - REG * s
-        sem = S["c%d_%d" % (idx[src], j)]
-        iq, isc = (T.rq[:, a + off:b + off], T.rs[:, a + off:b + off]) if from_stage else (T.wq[:, a:b], T.ws[:, a:b])
-        if nxt == partner[src]:
-            oq, osc = T.wq[:, a:b], T.ws[:, a:b]
+    def hop(src, K, nxt, from_stage):
+        ss = side[src]
+        off = REG * idx[src] - REG * ss
+        sem = S["c%d_%d" % (idx[src], K)]
+        final = nxt == partner[src]
+        en = _engines(topo.mask(core, nxt))
+        ps = CALLS[K]
+        w = len(en) // len(ps)
+        trs = []
+        for i, (kind, m0, m1) in enumerate(ps):
+            a, b = _cols(ss, m0, m1)
+            if from_stage:
+                ia = (T.rq if kind == "q" else T.rs)[:, a + off:b + off]
+            else:
+                ia = (T.wq if kind == "q" else T.ws)[:, a:b]
+            if final:
+                oa = (T.wq if kind == "q" else T.ws)[:, a:b]
+            else:
+                oa = (T.rq if kind == "q" else T.rs)[:, a + off:b + off]
+            if kind == "q":
+                ia, oa = ia.bitcast(u8), oa.bitcast(u8)
+            trs.append((ia, oa, _mk(en[i * w:(i + 1) * w])))
+            sent[0] += w
+        if len(trs) == 1:
+            rid, pid, _ = topo.addr(nxt)
+            g.remote_dma(out_ap=trs[0][1], in_ap=trs[0][0], remote_sem=sem, local_sem=S.sent, pid=pid, routing_id=rid,
+                         dma_engine_mask=trs[0][2])
         else:
-            oq, osc = T.rq[:, a + off:b + off], T.rs[:, a + off:b + off]
-        send(nxt, oq.bitcast(u8), iq.bitcast(u8), sem)
-        send(nxt, osc, isc, sem)
+            g.remote_dma_fused([RemoteDMATransfer(dst_ids=[did(nxt)], dma_engine_mask=m, remote_sem=sem, src=ia, dst=oa)
+                                for (ia, oa, m) in trs], local_sem=S.sent)
 
     def forward():
-        for (src, j, prev, nxt) in jobs:
-            g.wait_ge(S["c%d_%d" % (idx[src], j)], 2 * _nb(topo.mask(prev, core)))
-            hop(src, j, nxt, True)
+        for (src, K, prev, nxt) in jobs:
+            g.wait_ge(S["c%d_%d" % (idx[src], K)], _nb(topo.mask(prev, core)))
+            hop(src, K, nxt, True)
 
     if rank is None:
         forward()
@@ -152,105 +155,111 @@ def rank_program(g, core, T, topo):
     s, k = side[core], idx[core]
     o = 1 - s
     peers = [c for c in P["grp"][s] if c != core]
-    order = [(k + 1 + i) % 4 for i in range(4)]
+    order = [(k + 1 + i) % 4 for i in range(3)]
     te, ve, sc, sy = g.tensor, g.vector, g.scalar, g.sync
-    ksl = slice(NT * k, NT * k + NT)
-    ccnt = [2 * _nb(topo.mask(route[(partner[core], j)][-2], core)) for j in range(NCH)]
-    csem = [S["c%d_%d" % (k, j)] for j in range(NCH)]
+    R = 3 * NT
+    own = slice(R, R + NT)
+    ccnt = _nb(topo.mask(route[partner[core]][-2], core))
+    csem = [S["c%d_%d" % (k, K)] for K in range(NK)]
+    Relu = ActivationFunctionType.Relu
 
     sy.dma_start(T.xb[:], T.x[:]).then_inc(S.ld_x, 16)
     sc.dma_start(T.w2b[:], T.w2[:]).then_inc(S.ld_w2, 16)
-    for j in range(NCH):
-        t = _ctiles(s, j)
-        if t:
-            q = sy if j % 2 == 0 else sc
-            q.dma_start(T.w1b[:, 512 * t[0]:512 * t[1]], T.w1[:, 512 * t[0]:512 * t[1]]).then_inc(S["ld_w1_%d" % j], 16)
+    lt = []
+    for j, (m0, m1) in enumerate(LG):
+        t = [_utile(s, m) for m in range(m0, m1)]
+        lt.append((512 * min(t), 512 * (max(t) + 1)))
+        q = sc if j % 2 == 0 else sy
+        q.dma_start(T.w1b[:, lt[j][0]:lt[j][1]], T.w1[:, lt[j][0]:lt[j][1]]).then_inc(S["ld_w1_%d" % j], 16)
 
     ve.wait_ge(S.ld_w2, 16)
-    w2c = _ucol(s, 0)
+    w2c = _cols(s, 0, 1)[0]
     ve.quantize_mx(T.wq[:, w2c:w2c + NT], T.ws[:, w2c:w2c + NT], T.w2b[:]).then_inc(S.q_w2, 1)
     ve.wait_ge(S.ld_x, 16)
-    ve.quantize_mx(T.xq[:, ksl], T.xs[:, ksl], T.xb[:]).then_inc(S.q_x, 1)
-    for j in range(NCH):
-        t = _ctiles(s, j)
-        if t:
-            a = _ucol(s, 1) + NT * (t[0] - _utile(s, 1))
-            b = a + NT * (t[1] - t[0])
-            ve.wait_ge(S["ld_w1_%d" % j], 16)
-            ve.quantize_mx(T.wq[:, a:b], T.ws[:, a:b], T.w1b[:, 512 * t[0]:512 * t[1]]).then_inc(S["q_w1_%d" % j], 1)
+    ve.quantize_mx(T.xq[:, own], T.xs[:, own], T.xb[:]).then_inc(S.q_x, 1)
+    for j, (m0, m1) in enumerate(LG):
+        a, b = _cols(s, m0, m1)
+        ve.wait_ge(S["ld_w1_%d" % j], 16)
+        ve.quantize_mx(T.wq[:, a:b], T.ws[:, a:b], T.w1b[:, lt[j][0]:lt[j][1]]).then_inc(S["q_w1_%d" % j], 1)
 
+    def mm(bank, reg, m, x0, x1, sem):
+        col = _cols(reg, m, m + 1)[0]
+        te.matmul_mx(T.z[:, 512 * bank:512 * bank + (x1 - x0)], T.wq[:, col:col + NT], T.ws[:, col:col + NT],
+                     T.xq[:, x0:x1], T.xs[:, x0:x1], True, True).then_inc(sem, 1)
+
+    bankC, bankA, bankB, bankD, bankY = [4, 5, 6, 7], [0, 1, 2, 3], [4, 5, 6], [3, 7, 4, 5], 6
     te.wait_ge(S.q_x, 1)
+    for a in range(4):
+        te.wait_ge(S["q_w1_%d" % _group_of(a + 1)], 1)
+        mm(bankC[a], s, a + 1, R, R + NT, S["zC%d" % a])
     te.wait_ge(S.a_x, sum(2 * _nb(topo.mask(p, core)) for p in peers))
     for a in range(4):
-        te.wait_ge(S["q_w1_%d" % _chunk_of(a + 1)], 1)
-        col = _ucol(s, a + 1)
-        te.matmul_mx(T.z[:, 512 * a:512 * a + 512], T.wq[:, col:col + NT], T.ws[:, col:col + NT], T.xq[:], T.xs[:],
-                     True, True).then_inc(S["z0_%d" % a], 1)
+        mm(bankA[a], s, a + 1, 0, R, S["zA%d" % a])
+    te.wait_ge(S.afC, 4)
     for a in range(3):
-        j = _chunk_of(a + 1)
-        te.wait_ge(csem[j], ccnt[j])
-        col = _ucol(o, a + 1)
-        te.matmul_mx(T.z[:, 512 * (4 + a):512 * (4 + a) + 512], T.wq[:, col:col + NT], T.ws[:, col:col + NT],
-                     T.xq[:], T.xs[:], True, True).then_inc(S["z1_%d" % a], 1)
-    te.wait_ge(S.af0, 3)
-    for c in range(4):
-        te.wait_ge(S["al0_%d" % c], 1)
-    te.wait_ge(csem[NCH - 1], ccnt[NCH - 1])
-    col = _ucol(o, 4)
-    for i, c in enumerate(order):
-        te.matmul_mx(T.z[:, 512 * i:512 * i + NT], T.wq[:, col:col + NT], T.ws[:, col:col + NT],
-                     T.xq[:, NT * c:NT * c + NT], T.xs[:, NT * c:NT * c + NT], True, True).then_inc(S["zd%d" % i], 1)
+        for K in _need(a + 1):
+            te.wait_ge(csem[K], ccnt)
+        mm(bankB[a], o, a + 1, 0, R, S["zB%d" % a])
+    te.wait_ge(S.afA, 4)
+    for K in _need(4):
+        te.wait_ge(csem[K], ccnt)
+    for i in range(3):
+        mm(bankA[i], o, 4, NT * i, NT * i + NT, S["zL%d" % i])
+    for a in range(4):
+        if a == 2:
+            te.wait_ge(S.afB, 3)
+        mm(bankD[a], o, a + 1, R, R + NT, S["zD%d" % a])
 
-    for st in range(2):
-        hb, hq, hs = T["hb%d" % st], T["hq%d" % st], T["hs%d" % st]
-        reg = s if st == 0 else o
-        bank = 0 if st == 0 else 4
-        af = S["af%d" % st]
-        for a, eng in ((0, ve), (1, sc), (2, ve)):
-            b = _utile(reg, a + 1)
-            eng.wait_ge(S["z%d_%d" % (st, a)], 1)
-            zin = T.z[:, 512 * (bank + a):512 * (bank + a) + 512]
-            if eng is ve:
-                ve.tensor_scalar(hb[:, b:16 * NT:4], zin, 0.0, C, AluOpType.max, AluOpType.mult).then_inc(af, 1)
-            else:
-                sc.activation(hb[:, b:16 * NT:4], zin, ActivationFunctionType.Relu, scale=C).then_inc(af, 1)
-        b = _utile(reg, 4)
-        if st == 0:
-            sc.wait_ge(S.z0_3, 1)
-        for i, c in enumerate(order):
-            if st == 0:
-                zin = T.z[:, 512 * 3 + NT * c:512 * 3 + NT * c + NT]
-            else:
-                sc.wait_ge(S["zd%d" % i], 1)
-                zin = T.z[:, 512 * i:512 * i + NT]
-            sc.activation(hb[:, 512 * c + b:512 * c + 512:4], zin, ActivationFunctionType.Relu,
-                          scale=C).then_inc(S["al%d_%d" % (st, c)], 1)
-        ve.wait_ge(af, 3)
-        for c in order:
-            ve.wait_ge(S["al%d_%d" % (st, c)], 1)
-            ve.quantize_mx(hq[:, NT * c:NT * c + NT], hs[:, NT * c:NT * c + NT],
-                           hb[:, 512 * c:512 * c + 512]).then_inc(S["qh%d_%d" % (st, c)], 1)
+    def act(eng, hb, b, c0, c1, bank, zsem, asem):
+        eng.wait_ge(zsem, 1)
+        zin = T.z[:, 512 * bank:512 * bank + (c1 - c0)]
+        if eng is ve:
+            ve.tensor_scalar(hb[:, 4 * c0 + b:4 * c1:4], zin, 0.0, C, AluOpType.max, AluOpType.mult).then_inc(asem, 1)
+        else:
+            sc.activation(hb[:, 4 * c0 + b:4 * c1:4], zin, Relu, scale=C).then_inc(asem, 1)
 
-    full = topo.mask(core, peers[0])
-    eng = [e for e in range(full.bit_length()) if (full >> e) & 1]
-    n = len(eng)
+    def quant(st, c0, c1, sem):
+        ve.quantize_mx(T["hq%d" % st][:, c0:c1], T["hs%d" % st][:, c0:c1], T["hb%d" % st][:, 4 * c0:4 * c1]).then_inc(sem, 1)
 
-    def mk(lo, hi):
-        return sum(1 << e for e in eng[lo:hi])
-    mq = [mk(0, n // 2), mk(n // 2, 3 * n // 4), mk(3 * n // 4, n)]
-    ms = [mk(0, n // 4), mk(n // 4, n // 2), mk(n // 2, n)]
+    who = [ve, sc, ve, sc]
+    for a in range(4):
+        act(who[a], T.hb0, _utile(s, a + 1), R, R + NT, bankC[a], S["zC%d" % a], S.afC)
+    ve.wait_ge(S.afC, 4)
+    quant(0, R, R + NT, S.qhC)
+    for a in range(4):
+        act(who[a], T.hb0, _utile(s, a + 1), 0, R, bankA[a], S["zA%d" % a], S.afA)
+    ve.wait_ge(S.afA, 4)
+    quant(0, 0, R, S.qhA)
+    for a in range(3):
+        act(who[a], T.hb1, _utile(o, a + 1), 0, R, bankB[a], S["zB%d" % a], S.afB)
+    for i in range(3):
+        act(sc, T.hb1, _utile(o, 4), NT * i, NT * i + NT, bankA[i], S["zL%d" % i], S["aL%d" % i])
+    ve.wait_ge(S.afB, 3)
+    for i in range(3):
+        ve.wait_ge(S["aL%d" % i], 1)
+        quant(1, NT * i, NT * i + NT, S["qhB%d" % i])
+    for a in range(4):
+        act(who[a], T.hb1, _utile(o, a + 1), R, R + NT, bankD[a], S["zD%d" % a], S.afD)
+    ve.wait_ge(S.afD, 4)
+    quant(1, R, R + NT, S.qhD)
+
+    en = _engines(topo.mask(core, peers[0]))
+    n = len(en)
+    mq = [_mk(en[0:n // 2]), _mk(en[n // 2:3 * n // 4]), _mk(en[3 * n // 4:n])]
+    ms = [_mk(en[0:n // 4]), _mk(en[n // 4:n // 2]), _mk(en[n // 2:n])]
     hcnt = [_nb(mq[i]) + _nb(ms[i]) for i in range(3)]
 
-    yb = T.z[:, 512 * 7:512 * 7 + NT]
+    yb = T.z[:, 512 * bankY:512 * bankY + NT]
     L2 = []
-    xc = _ucol(o, 0)
-    L2.append(([(S.q_w2, 1), (S["qh0_%d" % k], 1)], T.wq[:, w2c:w2c + NT], T.ws[:, w2c:w2c + NT], T.hq0[:, ksl], T.hs0[:, ksl]))
+    xc = _cols(o, 0, 1)[0]
+    L2.append(([(S.q_w2, 1), (S.qhC, 1)], T.wq[:, w2c:w2c + NT], T.ws[:, w2c:w2c + NT], T.hq0[:, own], T.hs0[:, own]))
     for n_, pc in enumerate(peers):
         p = idx[pc]
         w = [(S.a_p, sum(2 * _nb(topo.mask(q, core)) for q in peers)), (S.a_ho, sum(hcnt))] if n_ == 0 else []
         a, h = 2 * NT * p + NT * s, 2 * NT * p
         L2.append((w, T.pq[:, a:a + NT], T.ps[:, a:a + NT], T.hin[:, h:h + NT], T.his[:, h:h + NT]))
-    L2.append(([(csem[0], ccnt[0]), (S["qh1_%d" % k], 1)], T.wq[:, xc:xc + NT], T.ws[:, xc:xc + NT], T.hq1[:, ksl], T.hs1[:, ksl]))
+    L2.append(([(csem[K], ccnt) for K in _need(0)] + [(S.qhD, 1)], T.wq[:, xc:xc + NT], T.ws[:, xc:xc + NT],
+               T.hq1[:, own], T.hs1[:, own]))
     for pc in peers:
         p = idx[pc]
         a, h = 2 * NT * p + NT * o, 2 * NT * p + NT
@@ -268,33 +277,37 @@ def rank_program(g, core, T, topo):
     sy.dma_start(T.y[:], T.ysb[:]).then_inc(S.y_st, 16)
     sy.wait_ge(S.y_st, 16)
 
-    for j in range(NCH):
-        if j == 0:
-            g.wait_ge(S.q_w2, 1)
-        if _ctiles(s, j):
-            g.wait_ge(S["q_w1_%d" % j], 1)
-        hop(core, j, route[(core, j)][1], False)
-        if j == 0:
+    g.wait_ge(S.q_w2, 1)
+    for K in range(NK):
+        if K == len(_need(0)):
             g.wait_ge(S.q_x, 1)
-            multi(peers, T.xq[:, ksl].bitcast(u8), T.xq[:, ksl].bitcast(u8), S.a_x)
-            multi(peers, T.xs[:, ksl], T.xs[:, ksl], S.a_x)
+            pos = [NT * ((k - idx[p] - 1) % 4) for p in peers]
+            multi(peers, [T.xq[:, a:a + NT].bitcast(u8) for a in pos], T.xq[:, own].bitcast(u8), S.a_x)
+            multi(peers, [T.xs[:, a:a + NT] for a in pos], T.xs[:, own], S.a_x)
+            for j in range(len(LG)):
+                g.wait_ge(S["q_w1_%d" % j], 1)
+        hop(core, K, route[core][1], False)
     forward()
-    g.wait_ge(csem[0], ccnt[0])
+    for K in _need(0):
+        g.wait_ge(csem[K], ccnt)
     pa = 2 * NT * k
-    multi(peers, T.pq[:, pa:pa + 2 * NT].bitcast(u8), T.wq[:, REG - NT:REG + NT].bitcast(u8), S.a_p)
-    multi(peers, T.ps[:, pa:pa + 2 * NT], T.ws[:, REG - NT:REG + NT], S.a_p)
+    multi(peers, [T.pq[:, pa:pa + 2 * NT].bitcast(u8)] * 3, T.wq[:, REG - NT:REG + NT].bitcast(u8), S.a_p)
+    multi(peers, [T.ps[:, pa:pa + 2 * NT]] * 3, T.ws[:, REG - NT:REG + NT], S.a_p)
     for st in range(2):
         hq, hs = T["hq%d" % st], T["hs%d" % st]
         rsem = S.a_ho if st == 0 else S["a_hc%d" % k]
-        for c in order[:3]:
-            g.wait_ge(S["qh%d_%d" % (st, c)], 1)
+        if st == 0:
+            g.wait_ge(S.qhA, 1)
+        else:
+            for i in range(3):
+                g.wait_ge(S["qhB%d" % i], 1)
         h = 2 * NT * k + NT * st
         g.remote_dma_fused([RemoteDMATransfer(dst_ids=[did(P["grp"][s][c])], dma_engine_mask=mq[i], remote_sem=rsem,
-                                              src=hq[:, NT * c:NT * c + NT].bitcast(u8),
+                                              src=hq[:, NT * i:NT * i + NT].bitcast(u8),
                                               dst=T.hin[:, h:h + NT].bitcast(u8))
-                            for i, c in enumerate(order[:3])], local_sem=S.sent)
+                            for i, c in enumerate(order)], local_sem=S.sent)
         g.remote_dma_fused([RemoteDMATransfer(dst_ids=[did(P["grp"][s][c])], dma_engine_mask=ms[i], remote_sem=rsem,
-                                              src=hs[:, NT * c:NT * c + NT], dst=T.his[:, h:h + NT])
-                            for i, c in enumerate(order[:3])], local_sem=S.sent)
+                                              src=hs[:, NT * i:NT * i + NT], dst=T.his[:, h:h + NT])
+                            for i, c in enumerate(order)], local_sem=S.sent)
         sent[0] += sum(hcnt)
     g.wait_ge(S.sent, sent[0])

@@ -5,8 +5,9 @@ from concourse.mybir import dt, AluOpType, ActivationFunctionType
 NT = 128
 G = 4
 REG = (G + 1) * NT
-CALLS = [[("q", 0, 1)], [("s", 0, 1)], [("q", 1, 2), ("s", 1, 5)], [("q", 2, 4)], [("q", 4, 5)]]
+CALLS = [[("s", 0, 1)], [("q", 0, 1)], [("q", 1, 2), ("s", 1, 5)], [("q", 2, 4)], [("q", 4, 5)]]
 NK = len(CALLS)
+MOVED = 0
 LG = [(1, 3), (3, 5)]
 C = float(np.float32(0.023))
 
@@ -62,6 +63,11 @@ def _group_of(m):
     return [j for j, (m0, m1) in enumerate(LG) if m0 <= m < m1][0]
 
 
+def _hop_engines(topo, a, b, K):
+    en = _engines(topo.mask(a, b))
+    return en[:len(en) // 2] if K in _need(0) and topo.chip(a) == topo.chip(b) else en
+
+
 def _plan(T, topo):
     cores = list(T.cores)
     chips = []
@@ -76,15 +82,20 @@ def _plan(T, topo):
     for s in (0, 1):
         free = [h for h in range(topo.CORES_PER_CHIP * topo.CHIPS)
                 if topo.chip(h) == chips[s] and h not in cores and topo.may_write(h, grp[1 - s][0])]
+        ported = [c for c in grp[s] if topo.may_write(c, partner[c])]
+        n = 0
         for c in grp[s]:
-            if topo.may_write(c, partner[c]):
-                route[c] = [c, partner[c]]
+            if c in ported:
+                route[c] = [[c, partner[c]]] * NK
             else:
                 free.sort(key=lambda h: topo.die(h) == topo.die(c))
-                route[c] = [c, free.pop(0), partner[c]]
+                first = free.pop(0)
+                late = ported[n % len(ported)] if ported else first
+                n += 1
+                route[c] = [[c, late if K >= NK - MOVED else first, partner[c]] for K in range(NK)]
     for K in range(NK):
         for c in cores:
-            p = route[c]
+            p = route[c][K]
             for k in range(1, len(p) - 1):
                 fwd.setdefault(p[k], []).append((c, K, p[k - 1], p[k + 1]))
     return {"grp": grp, "side": side, "idx": idx, "partner": partner, "route": route, "fwd": fwd}
@@ -116,7 +127,7 @@ def rank_program(g, core, T, topo):
         off = REG * idx[src] - REG * ss
         sem = S["c%d_%d" % (idx[src], K)]
         final = nxt == partner[src]
-        en = _engines(topo.mask(core, nxt))
+        en = _hop_engines(topo, core, nxt, K)
         ps = CALLS[K]
         w = len(en) // len(ps)
         trs = []
@@ -144,7 +155,7 @@ def rank_program(g, core, T, topo):
 
     def forward():
         for (src, K, prev, nxt) in jobs:
-            g.wait_ge(S["c%d_%d" % (idx[src], K)], _nb(topo.mask(prev, core)))
+            g.wait_ge(S["c%d_%d" % (idx[src], K)], len(_hop_engines(topo, prev, core, K)))
             hop(src, K, nxt, True)
 
     if rank is None:
@@ -159,12 +170,12 @@ def rank_program(g, core, T, topo):
     te, ve, sc, sy = g.tensor, g.vector, g.scalar, g.sync
     R = 3 * NT
     own = slice(R, R + NT)
-    ccnt = _nb(topo.mask(route[partner[core]][-2], core))
+    ccnt = [len(_hop_engines(topo, route[partner[core]][K][-2], core, K)) for K in range(NK)]
     csem = [S["c%d_%d" % (k, K)] for K in range(NK)]
     Relu = ActivationFunctionType.Relu
 
-    sy.dma_start(T.xb[:], T.x[:]).then_inc(S.ld_x, 16)
-    sc.dma_start(T.w2b[:], T.w2[:]).then_inc(S.ld_w2, 16)
+    sy.dma_start(T.w2b[:], T.w2[:]).then_inc(S.ld_w2, 16)
+    sc.dma_start(T.xb[:], T.x[:]).then_inc(S.ld_x, 16)
     lt = []
     for j, (m0, m1) in enumerate(LG):
         t = [_utile(s, m) for m in range(m0, m1)]
@@ -187,7 +198,8 @@ def rank_program(g, core, T, topo):
         te.matmul_mx(T.z[:, 512 * bank:512 * bank + (x1 - x0)], T.wq[:, col:col + NT], T.ws[:, col:col + NT],
                      T.xq[:, x0:x1], T.xs[:, x0:x1], True, True).then_inc(sem, 1)
 
-    bankC, bankA, bankB, bankD, bankY = [4, 5, 6, 7], [0, 1, 2, 3], [4, 5, 6], [3, 7, 4, 5], 6
+    bankC, bankA, bankB, bankD, bankY = [4, 5, 6, 7], [0, 1, 2, 3], [4, 5, 6], [3, 4, 5, 6], 7
+    yb = T.z[:, 512 * bankY:512 * bankY + NT]
     te.wait_ge(S.q_x, 1)
     for a in range(4):
         te.wait_ge(S["q_w1_%d" % _group_of(a + 1)], 1)
@@ -196,17 +208,20 @@ def rank_program(g, core, T, topo):
     for a in range(4):
         mm(bankA[a], s, a + 1, 0, R, S["zA%d" % a])
     te.wait_ge(S.afC, 4)
+    te.wait_ge(S.q_w2, 1)
+    te.wait_ge(S.qhC, 1)
+    te.matmul_mx(yb, T.wq[:, w2c:w2c + NT], T.ws[:, w2c:w2c + NT], T.hq0[:, own], T.hs0[:, own], True, False)
     for a in range(3):
         for K in _need(a + 1):
-            te.wait_ge(csem[K], ccnt)
+            te.wait_ge(csem[K], ccnt[K])
         mm(bankB[a], o, a + 1, 0, R, S["zB%d" % a])
     te.wait_ge(S.afA, 4)
     for K in _need(4):
-        te.wait_ge(csem[K], ccnt)
+        te.wait_ge(csem[K], ccnt[K])
     for i in range(3):
         mm(bankA[i], o, 4, NT * i, NT * i + NT, S["zL%d" % i])
     for a in range(4):
-        if a == 2:
+        if a == 1:
             te.wait_ge(S.afB, 3)
         mm(bankD[a], o, a + 1, R, R + NT, S["zD%d" % a])
 
@@ -249,26 +264,30 @@ def rank_program(g, core, T, topo):
     ms = [_mk(en[0:n // 4]), _mk(en[n // 4:n // 2]), _mk(en[n // 2:n])]
     hcnt = [_nb(mq[i]) + _nb(ms[i]) for i in range(3)]
 
-    yb = T.z[:, 512 * bankY:512 * bankY + NT]
     L2 = []
     xc = _cols(o, 0, 1)[0]
-    L2.append(([(S.q_w2, 1), (S.qhC, 1)], T.wq[:, w2c:w2c + NT], T.ws[:, w2c:w2c + NT], T.hq0[:, own], T.hs0[:, own]))
     for n_, pc in enumerate(peers):
         p = idx[pc]
         w = [(S.a_p, sum(2 * _nb(topo.mask(q, core)) for q in peers)), (S.a_ho, sum(hcnt))] if n_ == 0 else []
         a, h = 2 * NT * p + NT * s, 2 * NT * p
         L2.append((w, T.pq[:, a:a + NT], T.ps[:, a:a + NT], T.hin[:, h:h + NT], T.his[:, h:h + NT]))
-    L2.append(([(csem[K], ccnt) for K in _need(0)] + [(S.qhD, 1)], T.wq[:, xc:xc + NT], T.ws[:, xc:xc + NT],
-               T.hq1[:, own], T.hs1[:, own]))
-    for pc in peers:
+    hops = {pc: len(route[partner[pc]][0]) for pc in peers}
+    least = min(len(route[c_][0]) for c_ in route)
+
+    def far(pc):
         p = idx[pc]
         a, h = 2 * NT * p + NT * o, 2 * NT * p + NT
-        L2.append(([(S["a_hc%d" % p], hcnt[(k - p - 1) % 4])], T.pq[:, a:a + NT], T.ps[:, a:a + NT],
-                   T.hin[:, h:h + NT], T.his[:, h:h + NT]))
+        return ([(S["a_hc%d" % p], hcnt[(k - p - 1) % 4])], T.pq[:, a:a + NT], T.ps[:, a:a + NT],
+                T.hin[:, h:h + NT], T.his[:, h:h + NT])
+
+    L2 += [far(pc) for pc in peers if hops[pc] == least]
+    L2.append(([(csem[K], ccnt[K]) for K in _need(0)] + [(S.qhD, 1)], T.wq[:, xc:xc + NT], T.ws[:, xc:xc + NT],
+               T.hq1[:, own], T.hs1[:, own]))
+    L2 += [far(pc) for pc in peers if hops[pc] != least]
     for i, (w, wq_, ws_, hq_, hs_) in enumerate(L2):
         for sem, v in w:
             te.wait_ge(sem, v)
-        ins = te.matmul_mx(yb, wq_, ws_, hq_, hs_, i == 0, i == len(L2) - 1)
+        ins = te.matmul_mx(yb, wq_, ws_, hq_, hs_, False, i == len(L2) - 1)
         if i == len(L2) - 1:
             ins.then_inc(S.y_mm, 1)
     ve.wait_ge(S.y_mm, 1)
@@ -278,18 +297,21 @@ def rank_program(g, core, T, topo):
     sy.wait_ge(S.y_st, 16)
 
     g.wait_ge(S.q_w2, 1)
+    nw2 = len(_need(0))
+    x_at = nw2 + 1 if len(route[core][nw2]) > 2 else nw2
     for K in range(NK):
-        if K == len(_need(0)):
+        if K == x_at:
             g.wait_ge(S.q_x, 1)
             pos = [NT * ((k - idx[p] - 1) % 4) for p in peers]
             multi(peers, [T.xq[:, a:a + NT].bitcast(u8) for a in pos], T.xq[:, own].bitcast(u8), S.a_x)
             multi(peers, [T.xs[:, a:a + NT] for a in pos], T.xs[:, own], S.a_x)
+        if K == nw2:
             for j in range(len(LG)):
                 g.wait_ge(S["q_w1_%d" % j], 1)
-        hop(core, K, route[core][1], False)
+        hop(core, K, route[core][K][1], False)
     forward()
     for K in _need(0):
-        g.wait_ge(csem[K], ccnt)
+        g.wait_ge(csem[K], ccnt[K])
     pa = 2 * NT * k
     multi(peers, [T.pq[:, pa:pa + 2 * NT].bitcast(u8)] * 3, T.wq[:, REG - NT:REG + NT].bitcast(u8), S.a_p)
     multi(peers, [T.ps[:, pa:pa + 2 * NT]] * 3, T.ws[:, REG - NT:REG + NT], S.a_p)

@@ -7,7 +7,7 @@ G = 4
 REG = (G + 1) * NT
 CALLS = [[("s", 0, 1)], [("q", 0, 1)], [("q", 1, 2), ("s", 1, 5)], [("q", 2, 4)], [("q", 4, 5)]]
 NK = len(CALLS)
-MOVED = 0
+VIA_PEER = [1]
 LG = [(1, 3), (3, 5)]
 C = float(np.float32(0.023))
 
@@ -26,12 +26,13 @@ SCRATCH = {
     "ysb": ("sbuf", [128, NT], "float32"),
     "z": ("psum", [128, 8 * 512], "float32"),
 }
-SEMAPHORES = (["ld_x", "ld_w2", "q_x", "q_w2", "a_x", "a_p", "a_ho", "y_mm", "y_cp", "y_st", "sent",
-               "afC", "afA", "afB", "afD", "qhC", "qhA", "qhD"]
+SEMAPHORES = (["ld_x", "ld_w2", "q_x", "q_w2", "a_xe", "a_xl", "a_p", "a_ho", "y_mm", "y_cp", "y_st", "sent",
+               "afC", "afA0", "afA1", "afB", "afD", "qhC", "qhA", "qhD"]
               + ["ld_w1_%d" % j for j in range(len(LG))] + ["q_w1_%d" % j for j in range(len(LG))]
               + ["a_hc%d" % p for p in range(4)]
               + ["c%d_%d" % (i, j) for i in range(4) for j in range(NK)]
-              + ["z%s%d" % (ph, a) for ph in "CAD" for a in range(4)] + ["zB%d" % a for a in range(3)]
+              + ["z%s%d" % (ph, a) for ph in "CD" for a in range(4)] + ["zB%d" % a for a in range(3)]
+              + ["zA%d_%d" % (j, a) for j in range(2) for a in range(4)]
               + ["zL%d" % i for i in range(3)] + ["aL%d" % i for i in range(3)] + ["qhB%d" % i for i in range(3)])
 
 
@@ -65,7 +66,10 @@ def _group_of(m):
 
 def _hop_engines(topo, a, b, K):
     en = _engines(topo.mask(a, b))
-    return en[:len(en) // 2] if K in _need(0) and topo.chip(a) == topo.chip(b) else en
+    if K in _need(0) and topo.chip(a) == topo.chip(b):
+        h = len(en) // 2
+        return en[:h] if K == _need(0)[0] else en[h:]
+    return en
 
 
 def _plan(T, topo):
@@ -92,7 +96,7 @@ def _plan(T, topo):
                 first = free.pop(0)
                 late = ported[n % len(ported)] if ported else first
                 n += 1
-                route[c] = [[c, late if K >= NK - MOVED else first, partner[c]] for K in range(NK)]
+                route[c] = [[c, late if K in VIA_PEER else first, partner[c]] for K in range(NK)]
     for K in range(NK):
         for c in cores:
             p = route[c][K]
@@ -166,7 +170,20 @@ def rank_program(g, core, T, topo):
     s, k = side[core], idx[core]
     o = 1 - s
     peers = [c for c in P["grp"][s] if c != core]
-    order = [(k + 1 + i) % 4 for i in range(3)]
+    nw2 = len(_need(0))
+    gs = P["grp"][s]
+
+    def late(i):
+        return len(route[gs[i]][nw2]) > 2
+
+    def order_of(kk):
+        return sorted([i for i in range(4) if i != kk], key=lambda i: (late(i), (i - kk) % 4))
+
+    def posn(holder, tok):
+        return order_of(holder).index(tok)
+
+    order = order_of(k)
+    ne = len([i for i in order if not late(i)])
     te, ve, sc, sy = g.tensor, g.vector, g.scalar, g.sync
     R = 3 * NT
     own = slice(R, R + NT)
@@ -174,40 +191,58 @@ def rank_program(g, core, T, topo):
     csem = [S["c%d_%d" % (k, K)] for K in range(NK)]
     Relu = ActivationFunctionType.Relu
 
+    def load_x():
+        sc.dma_start(T.xb[:], T.x[:]).then_inc(S.ld_x, 16)
+
+    def quant_x():
+        ve.wait_ge(S.ld_x, 16)
+        ve.quantize_mx(T.xq[:, own], T.xs[:, own], T.xb[:]).then_inc(S.q_x, 1)
+
     sy.dma_start(T.w2b[:], T.w2[:]).then_inc(S.ld_w2, 16)
-    sc.dma_start(T.xb[:], T.x[:]).then_inc(S.ld_x, 16)
+    if not late(k):
+        load_x()
     lt = []
     for j, (m0, m1) in enumerate(LG):
         t = [_utile(s, m) for m in range(m0, m1)]
         lt.append((512 * min(t), 512 * (max(t) + 1)))
         q = sc if j % 2 == 0 else sy
         q.dma_start(T.w1b[:, lt[j][0]:lt[j][1]], T.w1[:, lt[j][0]:lt[j][1]]).then_inc(S["ld_w1_%d" % j], 16)
+    if late(k):
+        load_x()
 
     ve.wait_ge(S.ld_w2, 16)
     w2c = _cols(s, 0, 1)[0]
     ve.quantize_mx(T.wq[:, w2c:w2c + NT], T.ws[:, w2c:w2c + NT], T.w2b[:]).then_inc(S.q_w2, 1)
-    ve.wait_ge(S.ld_x, 16)
-    ve.quantize_mx(T.xq[:, own], T.xs[:, own], T.xb[:]).then_inc(S.q_x, 1)
+    if not late(k):
+        quant_x()
     for j, (m0, m1) in enumerate(LG):
         a, b = _cols(s, m0, m1)
         ve.wait_ge(S["ld_w1_%d" % j], 16)
         ve.quantize_mx(T.wq[:, a:b], T.ws[:, a:b], T.w1b[:, lt[j][0]:lt[j][1]]).then_inc(S["q_w1_%d" % j], 1)
+    if late(k):
+        quant_x()
 
     def mm(bank, reg, m, x0, x1, sem):
         col = _cols(reg, m, m + 1)[0]
         te.matmul_mx(T.z[:, 512 * bank:512 * bank + (x1 - x0)], T.wq[:, col:col + NT], T.ws[:, col:col + NT],
                      T.xq[:, x0:x1], T.xs[:, x0:x1], True, True).then_inc(sem, 1)
 
-    bankC, bankA, bankB, bankD, bankY = [4, 5, 6, 7], [0, 1, 2, 3], [4, 5, 6], [3, 4, 5, 6], 7
+    bankC, bankA, bankB, bankL, bankD, bankY = [4, 5, 6, 7], [[0, 1, 2, 3], [4, 5, 6, 7]], [0, 1, 2], [4, 5, 6], [7, 0, 1, 2], 3
+    xcnt = [sum(2 * _nb(topo.mask(gs[i], core)) for i in order if late(i) == bool(j)) for j in range(2)]
+    segs = [sg for sg in [(0, NT * ne, S.a_xe, xcnt[0]), (NT * ne, R, S.a_xl, xcnt[1])] if sg[1] > sg[0]]
     yb = T.z[:, 512 * bankY:512 * bankY + NT]
     te.wait_ge(S.q_x, 1)
     for a in range(4):
         te.wait_ge(S["q_w1_%d" % _group_of(a + 1)], 1)
         mm(bankC[a], s, a + 1, R, R + NT, S["zC%d" % a])
-    te.wait_ge(S.a_x, sum(2 * _nb(topo.mask(p, core)) for p in peers))
-    for a in range(4):
-        mm(bankA[a], s, a + 1, 0, R, S["zA%d" % a])
+    for j, (x0, x1, xsem, xn) in enumerate(segs):
+        te.wait_ge(xsem, xn)
+        if j == 1:
+            te.wait_ge(S.afC, 4)
+        for a in range(4):
+            mm(bankA[j][a], s, a + 1, x0, x1, S["zA%d_%d" % (j, a)])
     te.wait_ge(S.afC, 4)
+    te.wait_ge(S.afA0, 4)
     te.wait_ge(S.q_w2, 1)
     te.wait_ge(S.qhC, 1)
     te.matmul_mx(yb, T.wq[:, w2c:w2c + NT], T.ws[:, w2c:w2c + NT], T.hq0[:, own], T.hs0[:, own], True, False)
@@ -215,11 +250,12 @@ def rank_program(g, core, T, topo):
         for K in _need(a + 1):
             te.wait_ge(csem[K], ccnt[K])
         mm(bankB[a], o, a + 1, 0, R, S["zB%d" % a])
-    te.wait_ge(S.afA, 4)
+    if len(segs) > 1:
+        te.wait_ge(S.afA1, 4)
     for K in _need(4):
         te.wait_ge(csem[K], ccnt[K])
     for i in range(3):
-        mm(bankA[i], o, 4, NT * i, NT * i + NT, S["zL%d" % i])
+        mm(bankL[i], o, 4, NT * i, NT * i + NT, S["zL%d" % i])
     for a in range(4):
         if a == 1:
             te.wait_ge(S.afB, 3)
@@ -241,14 +277,16 @@ def rank_program(g, core, T, topo):
         act(who[a], T.hb0, _utile(s, a + 1), R, R + NT, bankC[a], S["zC%d" % a], S.afC)
     ve.wait_ge(S.afC, 4)
     quant(0, R, R + NT, S.qhC)
-    for a in range(4):
-        act(who[a], T.hb0, _utile(s, a + 1), 0, R, bankA[a], S["zA%d" % a], S.afA)
-    ve.wait_ge(S.afA, 4)
+    for j, (x0, x1, _, _) in enumerate(segs):
+        for a in range(4):
+            act(who[a], T.hb0, _utile(s, a + 1), x0, x1, bankA[j][a], S["zA%d_%d" % (j, a)], S["afA%d" % j])
+    for j in range(len(segs)):
+        ve.wait_ge(S["afA%d" % j], 4)
     quant(0, 0, R, S.qhA)
     for a in range(3):
         act(who[a], T.hb1, _utile(o, a + 1), 0, R, bankB[a], S["zB%d" % a], S.afB)
     for i in range(3):
-        act(sc, T.hb1, _utile(o, 4), NT * i, NT * i + NT, bankA[i], S["zL%d" % i], S["aL%d" % i])
+        act(sc, T.hb1, _utile(o, 4), NT * i, NT * i + NT, bankL[i], S["zL%d" % i], S["aL%d" % i])
     ve.wait_ge(S.afB, 3)
     for i in range(3):
         ve.wait_ge(S["aL%d" % i], 1)
@@ -268,7 +306,8 @@ def rank_program(g, core, T, topo):
     xc = _cols(o, 0, 1)[0]
     for n_, pc in enumerate(peers):
         p = idx[pc]
-        w = [(S.a_p, sum(2 * _nb(topo.mask(q, core)) for q in peers)), (S.a_ho, sum(hcnt))] if n_ == 0 else []
+        w = [(S.a_p, sum(2 * _nb(topo.mask(q, core)) for q in peers)),
+             (S.a_ho, sum(hcnt[posn(idx[q], k)] for q in peers))] if n_ == 0 else []
         a, h = 2 * NT * p + NT * s, 2 * NT * p
         L2.append((w, T.pq[:, a:a + NT], T.ps[:, a:a + NT], T.hin[:, h:h + NT], T.his[:, h:h + NT]))
     hops = {pc: len(route[partner[pc]][0]) for pc in peers}
@@ -277,7 +316,7 @@ def rank_program(g, core, T, topo):
     def far(pc):
         p = idx[pc]
         a, h = 2 * NT * p + NT * o, 2 * NT * p + NT
-        return ([(S["a_hc%d" % p], hcnt[(k - p - 1) % 4])], T.pq[:, a:a + NT], T.ps[:, a:a + NT],
+        return ([(S["a_hc%d" % p], hcnt[posn(p, k)])], T.pq[:, a:a + NT], T.ps[:, a:a + NT],
                 T.hin[:, h:h + NT], T.his[:, h:h + NT])
 
     L2 += [far(pc) for pc in peers if hops[pc] == least]
@@ -297,19 +336,20 @@ def rank_program(g, core, T, topo):
     sy.wait_ge(S.y_st, 16)
 
     g.wait_ge(S.q_w2, 1)
-    nw2 = len(_need(0))
-    x_at = nw2 + 1 if len(route[core][nw2]) > 2 else nw2
+    x_at = nw2 + 2 if late(k) else nw2
     for K in range(NK):
         if K == x_at:
             g.wait_ge(S.q_x, 1)
-            pos = [NT * ((k - idx[p] - 1) % 4) for p in peers]
-            multi(peers, [T.xq[:, a:a + NT].bitcast(u8) for a in pos], T.xq[:, own].bitcast(u8), S.a_x)
-            multi(peers, [T.xs[:, a:a + NT] for a in pos], T.xs[:, own], S.a_x)
+            pos = [NT * posn(idx[p], k) for p in peers]
+            xsem = S.a_xl if late(k) else S.a_xe
+            multi(peers, [T.xq[:, a:a + NT].bitcast(u8) for a in pos], T.xq[:, own].bitcast(u8), xsem)
+            multi(peers, [T.xs[:, a:a + NT] for a in pos], T.xs[:, own], xsem)
         if K == nw2:
             for j in range(len(LG)):
                 g.wait_ge(S["q_w1_%d" % j], 1)
         hop(core, K, route[core][K][1], False)
-    forward()
+        if K == nw2:
+            forward()
     for K in _need(0):
         g.wait_ge(csem[K], ccnt[K])
     pa = 2 * NT * k

import numpy as np
from concourse.bass import DstId, RemoteDMATransfer
from concourse.mybir import dt, AluOpType, ActivationFunctionType

NT = 128
G = 4
REG = (G + 1) * NT
CALLS = [[("s", 0, 1)], [("q", 0, 1)], [("q", 1, 2), ("s", 1, 5)], [("q", 2, 4)], [("q", 4, 5)]]
NK = len(CALLS)
VIA_PEER = [1]
LG = [(1, 3), (3, 5)]
C = float(np.float32(0.023))

SCRATCH = {
    "xb": ("sbuf", [128, 4 * NT], "bfloat16"),
    "w2b": ("sbuf", [128, 4 * NT], "bfloat16"),
    "w1b": ("sbuf", [128, 4 * NT * G], "bfloat16"),
    "xq": ("sbuf", [128, 4 * NT], "float8_e4m3fn_x4"), "xs": ("sbuf", [128, 4 * NT], "uint8"),
    "wq": ("sbuf", [128, 2 * REG], "float8_e4m3fn_x4"), "ws": ("sbuf", [128, 2 * REG], "uint8"),
    "rq": ("sbuf", [128, 4 * REG], "float8_e4m3fn_x4"), "rs": ("sbuf", [128, 4 * REG], "uint8"),
    "pq": ("sbuf", [128, 8 * NT], "float8_e4m3fn_x4"), "ps": ("sbuf", [128, 8 * NT], "uint8"),
    "hb0": ("sbuf", [128, 16 * NT], "bfloat16"), "hb1": ("sbuf", [128, 16 * NT], "bfloat16"),
    "hq0": ("sbuf", [128, 4 * NT], "float8_e4m3fn_x4"), "hs0": ("sbuf", [128, 4 * NT], "uint8"),
    "hq1": ("sbuf", [128, 4 * NT], "float8_e4m3fn_x4"), "hs1": ("sbuf", [128, 4 * NT], "uint8"),
    "hin": ("sbuf", [128, 8 * NT], "float8_e4m3fn_x4"), "his": ("sbuf", [128, 8 * NT], "uint8"),
    "ysb": ("sbuf", [128, NT], "float32"),
    "z": ("psum", [128, 8 * 512], "float32"),
}
SEMAPHORES = (["ld_x", "ld_w2", "q_x", "q_w2", "a_xe", "a_xl", "a_p", "a_ho", "y_mm", "y_cp", "y_st", "sent",
               "afC", "afA0", "afA1", "afB", "afD", "qhC", "qhA", "qhD"]
              + ["ld_w1_%d" % j for j in range(len(LG))] + ["q_w1_%d" % j for j in range(len(LG))]
              + ["a_hc%d" % p for p in range(4)]
              + ["c%d_%d" % (i, j) for i in range(4) for j in range(NK)]
              + ["z%s%d" % (ph, a) for ph in "CD" for a in range(4)] + ["zB%d" % a for a in range(3)]
              + ["zA%d_%d" % (j, a) for j in range(2) for a in range(4)]
              + ["zL%d" % i for i in range(3)] + ["aL%d" % i for i in range(3)] + ["qhB%d" % i for i in range(3)])


def _nb(m):
    return bin(m).count("1")


def _engines(m):
    return [e for e in range(m.bit_length()) if (m >> e) & 1]


def _mk(es):
    return sum(1 << e for e in es)


def _cols(s, m0, m1):
    return (REG - NT * m1, REG - NT * m0) if s == 0 else (REG + NT * m0, REG + NT * m1)


def _utile(s, m):
    return G - m if s == 0 else m - 1


def _need(m):
    return [K for K, ps in enumerate(CALLS) if any(m0 <= m < m1 for (_, m0, m1) in ps)]


def _group_of(m):
    return [j for j, (m0, m1) in enumerate(LG) if m0 <= m < m1][0]


def _hop_engines(topo, a, b, K):
    en = _engines(topo.mask(a, b))
    if K in _need(0) and topo.chip(a) == topo.chip(b):
        h = len(en) // 2
        return en[:h] if K == _need(0)[0] else en[h:]
    return en


def _plan(T, topo):
    cores = list(T.cores)
    chips = []
    for c in cores:
        if topo.chip(c) not in chips:
            chips.append(topo.chip(c))
    grp = [[c for c in cores if topo.chip(c) == ch] for ch in chips]
    side, idx, partner, route, fwd = {}, {}, {}, {}, {}
    for s in (0, 1):
        for i, c in enumerate(grp[s]):
            side[c], idx[c], partner[c] = s, i, grp[1 - s][i]
    for s in (0, 1):
        free = [h for h in range(topo.CORES_PER_CHIP * topo.CHIPS)
                if topo.chip(h) == chips[s] and h not in cores and topo.may_write(h, grp[1 - s][0])]
        ported = [c for c in grp[s] if topo.may_write(c, partner[c])]
        n = 0
        for c in grp[s]:
            if c in ported:
                route[c] = [[c, partner[c]]] * NK
            else:
                free.sort(key=lambda h: topo.die(h) == topo.die(c))
                first = free.pop(0)
                late = ported[n % len(ported)] if ported else first
                n += 1
                route[c] = [[c, late if K in VIA_PEER else first, partner[c]] for K in range(NK)]
    for K in range(NK):
        for c in cores:
            p = route[c][K]
            for k in range(1, len(p) - 1):
                fwd.setdefault(p[k], []).append((c, K, p[k - 1], p[k + 1]))
    return {"grp": grp, "side": side, "idx": idx, "partner": partner, "route": route, "fwd": fwd}


def rank_program(g, core, T, topo):
    P = _plan(T, topo)
    side, idx, partner, route = P["side"], P["idx"], P["partner"], P["route"]
    jobs = P["fwd"].get(core, [])
    rank = T.rank_of(core)
    if rank is None and not jobs:
        return
    S = T.sem
    u8 = dt.uint8
    sent = [0]

    def did(d):
        rid, pid, _ = topo.addr(d)
        return DstId(rid=rid, pnc=pid)

    def multi(dsts, out_aps, in_ap, rsem):
        m = topo.mask(core, dsts[0])
        g.remote_dma_fused([RemoteDMATransfer(dst_ids=[did(d) for d in dsts], dma_engine_mask=m, remote_sem=rsem,
                                              srcs=[in_ap], dsts=out_aps)], local_sem=S.sent)
        sent[0] += _nb(m)

    def hop(src, K, nxt, from_stage):
        ss = side[src]
        off = REG * idx[src] - REG * ss
        sem = S["c%d_%d" % (idx[src], K)]
        final = nxt == partner[src]
        en = _hop_engines(topo, core, nxt, K)
        ps = CALLS[K]
        w = len(en) // len(ps)
        trs = []
        for i, (kind, m0, m1) in enumerate(ps):
            a, b = _cols(ss, m0, m1)
            if from_stage:
                ia = (T.rq if kind == "q" else T.rs)[:, a + off:b + off]
            else:
                ia = (T.wq if kind == "q" else T.ws)[:, a:b]
            if final:
                oa = (T.wq if kind == "q" else T.ws)[:, a:b]
            else:
                oa = (T.rq if kind == "q" else T.rs)[:, a + off:b + off]
            if kind == "q":
                ia, oa = ia.bitcast(u8), oa.bitcast(u8)
            trs.append((ia, oa, _mk(en[i * w:(i + 1) * w])))
            sent[0] += w
        if len(trs) == 1:
            rid, pid, _ = topo.addr(nxt)
            g.remote_dma(out_ap=trs[0][1], in_ap=trs[0][0], remote_sem=sem, local_sem=S.sent, pid=pid, routing_id=rid,
                         dma_engine_mask=trs[0][2])
        else:
            g.remote_dma_fused([RemoteDMATransfer(dst_ids=[did(nxt)], dma_engine_mask=m, remote_sem=sem, src=ia, dst=oa)
                                for (ia, oa, m) in trs], local_sem=S.sent)

    def forward():
        for (src, K, prev, nxt) in jobs:
            g.wait_ge(S["c%d_%d" % (idx[src], K)], len(_hop_engines(topo, prev, core, K)))
            hop(src, K, nxt, True)

    if rank is None:
        forward()
        g.wait_ge(S.sent, sent[0])
        return

    s, k = side[core], idx[core]
    o = 1 - s
    peers = [c for c in P["grp"][s] if c != core]
    nw2 = len(_need(0))
    gs = P["grp"][s]

    def late(i):
        return len(route[gs[i]][nw2]) > 2

    def order_of(kk):
        return sorted([i for i in range(4) if i != kk], key=lambda i: (late(i), (i - kk) % 4))

    def posn(holder, tok):
        return order_of(holder).index(tok)

    order = order_of(k)
    ne = len([i for i in order if not late(i)])
    te, ve, sc, sy = g.tensor, g.vector, g.scalar, g.sync
    R = 3 * NT
    own = slice(R, R + NT)
    ccnt = [len(_hop_engines(topo, route[partner[core]][K][-2], core, K)) for K in range(NK)]
    csem = [S["c%d_%d" % (k, K)] for K in range(NK)]
    Relu = ActivationFunctionType.Relu

    def load_x():
        sc.dma_start(T.xb[:], T.x[:]).then_inc(S.ld_x, 16)

    def quant_x():
        ve.wait_ge(S.ld_x, 16)
        ve.quantize_mx(T.xq[:, own], T.xs[:, own], T.xb[:]).then_inc(S.q_x, 1)

    sy.dma_start(T.w2b[:], T.w2[:]).then_inc(S.ld_w2, 16)
    if not late(k):
        load_x()
    lt = []
    for j, (m0, m1) in enumerate(LG):
        t = [_utile(s, m) for m in range(m0, m1)]
        lt.append((512 * min(t), 512 * (max(t) + 1)))
        q = sc if j % 2 == 0 else sy
        q.dma_start(T.w1b[:, lt[j][0]:lt[j][1]], T.w1[:, lt[j][0]:lt[j][1]]).then_inc(S["ld_w1_%d" % j], 16)
    if late(k):
        load_x()

    ve.wait_ge(S.ld_w2, 16)
    w2c = _cols(s, 0, 1)[0]
    ve.quantize_mx(T.wq[:, w2c:w2c + NT], T.ws[:, w2c:w2c + NT], T.w2b[:]).then_inc(S.q_w2, 1)
    if not late(k):
        quant_x()
    for j, (m0, m1) in enumerate(LG):
        a, b = _cols(s, m0, m1)
        ve.wait_ge(S["ld_w1_%d" % j], 16)
        ve.quantize_mx(T.wq[:, a:b], T.ws[:, a:b], T.w1b[:, lt[j][0]:lt[j][1]]).then_inc(S["q_w1_%d" % j], 1)
    if late(k):
        quant_x()

    def mm(bank, reg, m, x0, x1, sem):
        col = _cols(reg, m, m + 1)[0]
        te.matmul_mx(T.z[:, 512 * bank:512 * bank + (x1 - x0)], T.wq[:, col:col + NT], T.ws[:, col:col + NT],
                     T.xq[:, x0:x1], T.xs[:, x0:x1], True, True).then_inc(sem, 1)

    bankC, bankA, bankB, bankL, bankD, bankY = [4, 5, 6, 7], [[0, 1, 2, 3], [4, 5, 6, 7]], [0, 1, 2], [4, 5, 6], [7, 0, 1, 2], 3
    xcnt = [sum(2 * _nb(topo.mask(gs[i], core)) for i in order if late(i) == bool(j)) for j in range(2)]
    segs = [sg for sg in [(0, NT * ne, S.a_xe, xcnt[0]), (NT * ne, R, S.a_xl, xcnt[1])] if sg[1] > sg[0]]
    yb = T.z[:, 512 * bankY:512 * bankY + NT]
    te.wait_ge(S.q_x, 1)
    for a in range(4):
        te.wait_ge(S["q_w1_%d" % _group_of(a + 1)], 1)
        mm(bankC[a], s, a + 1, R, R + NT, S["zC%d" % a])
    for j, (x0, x1, xsem, xn) in enumerate(segs):
        te.wait_ge(xsem, xn)
        if j == 1:
            te.wait_ge(S.afC, 4)
        for a in range(4):
            mm(bankA[j][a], s, a + 1, x0, x1, S["zA%d_%d" % (j, a)])
    te.wait_ge(S.afC, 4)
    te.wait_ge(S.afA0, 4)
    te.wait_ge(S.q_w2, 1)
    te.wait_ge(S.qhC, 1)
    te.matmul_mx(yb, T.wq[:, w2c:w2c + NT], T.ws[:, w2c:w2c + NT], T.hq0[:, own], T.hs0[:, own], True, False)
    for a in range(3):
        for K in _need(a + 1):
            te.wait_ge(csem[K], ccnt[K])
        mm(bankB[a], o, a + 1, 0, R, S["zB%d" % a])
    if len(segs) > 1:
        te.wait_ge(S.afA1, 4)
    for K in _need(4):
        te.wait_ge(csem[K], ccnt[K])
    for i in range(3):
        mm(bankL[i], o, 4, NT * i, NT * i + NT, S["zL%d" % i])
    for a in range(4):
        if a == 1:
            te.wait_ge(S.afB, 3)
        mm(bankD[a], o, a + 1, R, R + NT, S["zD%d" % a])

    def act(eng, hb, b, c0, c1, bank, zsem, asem):
        eng.wait_ge(zsem, 1)
        zin = T.z[:, 512 * bank:512 * bank + (c1 - c0)]
        if eng is ve:
            ve.tensor_scalar(hb[:, 4 * c0 + b:4 * c1:4], zin, 0.0, C, AluOpType.max, AluOpType.mult).then_inc(asem, 1)
        else:
            sc.activation(hb[:, 4 * c0 + b:4 * c1:4], zin, Relu, scale=C).then_inc(asem, 1)

    def quant(st, c0, c1, sem):
        ve.quantize_mx(T["hq%d" % st][:, c0:c1], T["hs%d" % st][:, c0:c1], T["hb%d" % st][:, 4 * c0:4 * c1]).then_inc(sem, 1)

    who = [ve, sc, ve, sc]
    for a in range(4):
        act(who[a], T.hb0, _utile(s, a + 1), R, R + NT, bankC[a], S["zC%d" % a], S.afC)
    ve.wait_ge(S.afC, 4)
    quant(0, R, R + NT, S.qhC)
    for j, (x0, x1, _, _) in enumerate(segs):
        for a in range(4):
            act(who[a], T.hb0, _utile(s, a + 1), x0, x1, bankA[j][a], S["zA%d_%d" % (j, a)], S["afA%d" % j])
    for j in range(len(segs)):
        ve.wait_ge(S["afA%d" % j], 4)
    quant(0, 0, R, S.qhA)
    for a in range(3):
        act(who[a], T.hb1, _utile(o, a + 1), 0, R, bankB[a], S["zB%d" % a], S.afB)
    for i in range(3):
        act(sc, T.hb1, _utile(o, 4), NT * i, NT * i + NT, bankL[i], S["zL%d" % i], S["aL%d" % i])
    ve.wait_ge(S.afB, 3)
    for i in range(3):
        ve.wait_ge(S["aL%d" % i], 1)
        quant(1, NT * i, NT * i + NT, S["qhB%d" % i])
    for a in range(4):
        act(who[a], T.hb1, _utile(o, a + 1), R, R + NT, bankD[a], S["zD%d" % a], S.afD)
    ve.wait_ge(S.afD, 4)
    quant(1, R, R + NT, S.qhD)

    en = _engines(topo.mask(core, peers[0]))
    n = len(en)
    mq = [_mk(en[0:n // 2]), _mk(en[n // 2:3 * n // 4]), _mk(en[3 * n // 4:n])]
    ms = [_mk(en[0:n // 4]), _mk(en[n // 4:n // 2]), _mk(en[n // 2:n])]
    hcnt = [_nb(mq[i]) + _nb(ms[i]) for i in range(3)]

    L2 = []
    xc = _cols(o, 0, 1)[0]
    for n_, pc in enumerate(peers):
        p = idx[pc]
        w = [(S.a_p, sum(2 * _nb(topo.mask(q, core)) for q in peers)),
             (S.a_ho, sum(hcnt[posn(idx[q], k)] for q in peers))] if n_ == 0 else []
        a, h = 2 * NT * p + NT * s, 2 * NT * p
        L2.append((w, T.pq[:, a:a + NT], T.ps[:, a:a + NT], T.hin[:, h:h + NT], T.his[:, h:h + NT]))
    hops = {pc: len(route[partner[pc]][0]) for pc in peers}
    least = min(len(route[c_][0]) for c_ in route)

    def far(pc):
        p = idx[pc]
        a, h = 2 * NT * p + NT * o, 2 * NT * p + NT
        return ([(S["a_hc%d" % p], hcnt[posn(p, k)])], T.pq[:, a:a + NT], T.ps[:, a:a + NT],
                T.hin[:, h:h + NT], T.his[:, h:h + NT])

    L2 += [far(pc) for pc in peers if hops[pc] == least]
    L2.append(([(csem[K], ccnt[K]) for K in _need(0)] + [(S.qhD, 1)], T.wq[:, xc:xc + NT], T.ws[:, xc:xc + NT],
               T.hq1[:, own], T.hs1[:, own]))
    L2 += [far(pc) for pc in peers if hops[pc] != least]
    for i, (w, wq_, ws_, hq_, hs_) in enumerate(L2):
        for sem, v in w:
            te.wait_ge(sem, v)
        ins = te.matmul_mx(yb, wq_, ws_, hq_, hs_, False, i == len(L2) - 1)
        if i == len(L2) - 1:
            ins.then_inc(S.y_mm, 1)
    ve.wait_ge(S.y_mm, 1)
    ve.tensor_copy(T.ysb[:], yb).then_inc(S.y_cp, 1)
    sy.wait_ge(S.y_cp, 1)
    sy.dma_start(T.y[:], T.ysb[:]).then_inc(S.y_st, 16)
    sy.wait_ge(S.y_st, 16)

    g.wait_ge(S.q_w2, 1)
    x_at = nw2 + 2 if late(k) else nw2
    for K in range(NK):
        if K == x_at:
            g.wait_ge(S.q_x, 1)
            pos = [NT * posn(idx[p], k) for p in peers]
            xsem = S.a_xl if late(k) else S.a_xe
            multi(peers, [T.xq[:, a:a + NT].bitcast(u8) for a in pos], T.xq[:, own].bitcast(u8), xsem)
            multi(peers, [T.xs[:, a:a + NT] for a in pos], T.xs[:, own], xsem)
        if K == nw2:
            for j in range(len(LG)):
                g.wait_ge(S["q_w1_%d" % j], 1)
        hop(core, K, route[core][K][1], False)
        if K == nw2:
            forward()
    for K in _need(0):
        g.wait_ge(csem[K], ccnt[K])
    pa = 2 * NT * k
    multi(peers, [T.pq[:, pa:pa + 2 * NT].bitcast(u8)] * 3, T.wq[:, REG - NT:REG + NT].bitcast(u8), S.a_p)
    multi(peers, [T.ps[:, pa:pa + 2 * NT]] * 3, T.ws[:, REG - NT:REG + NT], S.a_p)
    for st in range(2):
        hq, hs = T["hq%d" % st], T["hs%d" % st]
        rsem = S.a_ho if st == 0 else S["a_hc%d" % k]
        if st == 0:
            g.wait_ge(S.qhA, 1)
        else:
            for i in range(3):
                g.wait_ge(S["qhB%d" % i], 1)
        h = 2 * NT * k + NT * st
        g.remote_dma_fused([RemoteDMATransfer(dst_ids=[did(P["grp"][s][c])], dma_engine_mask=mq[i], remote_sem=rsem,
                                              src=hq[:, NT * i:NT * i + NT].bitcast(u8),
                                              dst=T.hin[:, h:h + NT].bitcast(u8))
                            for i, c in enumerate(order)], local_sem=S.sent)
        g.remote_dma_fused([RemoteDMATransfer(dst_ids=[did(P["grp"][s][c])], dma_engine_mask=ms[i], remote_sem=rsem,
                                              src=hs[:, NT * i:NT * i + NT], dst=T.his[:, h:h + NT])
                            for i, c in enumerate(order)], local_sem=S.sent)
        sent[0] += sum(hcnt)
    g.wait_ge(S.sent, sent[0])
